import numpy as np
import ml_dtypes


def mxq(x, axis, fmt="e4m3"):
    dtype, down = {"e4m3": (ml_dtypes.float8_e4m3fn, 7), "e5m2": (ml_dtypes.float8_e5m2, 14)}[fmt]
    v = np.moveaxis(np.asarray(x, np.float32).astype(ml_dtypes.bfloat16).astype(np.float64), axis, -1)
    blocks = v.reshape(v.shape[:-1] + (-1, 32))
    amax = np.abs(blocks).max(-1, keepdims=True)
    byte = np.maximum(np.where(amax > 0, np.frexp(amax)[1] - 1 + 127, 0) - down, 1)
    scale = np.exp2(byte - 127.0)
    codes = (blocks / scale).astype(np.float32).astype(dtype).astype(np.float64)
    return np.moveaxis((codes * scale).reshape(v.shape), -1, axis)


WIDE = False


def mx_kscale(k):
    if not WIDE:
        return np.ones(k)
    levels = np.array([10, -10, 5, -5, 0])
    if k % 512:
        return np.exp2(np.random.permutation(np.resize(levels, k // 32))).repeat(32)
    a = np.empty((k // 512, 16))
    for p in range(k // 512):
        a[p, :8] = np.random.permutation(np.resize(levels, 8))
        for g in range(8):
            far = levels[np.abs(levels - a[p, g]) >= 10]
            a[p, g + 8] = far[np.random.randint(len(far))]
    return np.exp2(a.ravel()).repeat(32)


def f64(x):
    return np.asarray(x).astype(np.float64)


def striped(idx):
    return np.tile(idx.reshape(-1, 16).T, (8, 1)).astype(np.uint16)


def unstriped(offs):
    return offs[:16].T.reshape(-1).astype(np.int64)


E2M1 = np.array([0.0, 0.5, 1.0, 1.5, 2.0, 3.0, 4.0, 6.0, -0.0, -0.5, -1.0, -1.5, -2.0, -3.0, -4.0, -6.0])


def pack_weight(w, fmt):
    k, n = w.shape
    w = f64(np.asarray(w, np.float32).astype(ml_dtypes.bfloat16)).reshape(k // 32, 32, n)
    amax = np.abs(w).max(1)
    if fmt == "e4m3":
        byte = np.frexp(amax)[1] - 1 + 127 - 7
    else:
        mant, ex = np.frexp(amax / 6.0)
        byte = np.where(mant > 0.5, ex, ex - 1) + 127
    byte = np.clip(np.where(amax > 0, byte, 1), 1, 254)
    scaled = (w * np.exp2(127.0 - byte)[:, None, :]).reshape(k, n).astype(np.float32)
    by_word = np.ascontiguousarray(scaled.reshape(k // 512, 128, 4, n).transpose(0, 1, 3, 2))
    if fmt == "e4m3":
        words = by_word.astype(ml_dtypes.float8_e4m3fn).view(np.uint8)
    else:
        c = by_word.astype(ml_dtypes.float4_e2m1fn).view(np.uint8) & 0xF
        words = (c[..., 0::2] | (c[..., 1::2] << 4)).reshape(k // 512, 128, 2 * n)
    return np.ascontiguousarray(words), np.ascontiguousarray(byte.astype(np.uint8).reshape(k // 512, 16, n))


def unpack_weight(words, scales, fmt):
    g, _, n = scales.shape
    words = np.ascontiguousarray(words).reshape(g, 128, n, -1)
    if fmt == "e4m3":
        vals = words.view(ml_dtypes.float8_e4m3fn).astype(np.float64)
    else:
        nib = np.empty((g, 128, n, 4), np.uint8)
        nib[..., 0::2] = words & 0xF
        nib[..., 1::2] = words >> 4
        vals = E2M1[nib]
    vals = vals * np.repeat(np.exp2(scales.astype(np.float64) - 127.0), 8, axis=1)[..., None]
    return vals.transpose(0, 1, 3, 2).reshape(g * 512, n)


def gelu(v):
    return 0.5 * v * (1.0 + np.tanh(np.sqrt(2.0 / np.pi) * (v + 0.044715 * v**3)))


def striped8(idx):
    return np.concatenate([v.reshape(-1, 16).T for v in idx]).astype(np.uint16)


def unstriped8(offs):
    return np.stack([offs[16 * g:16 * g + 16].T.reshape(-1) for g in range(8)]).astype(np.int64)


def heads(h, wgt, idx8):
    r = np.arange(h.shape[0])
    return wgt[r // 4 % 128] * h[r[:, None], idx8[r % 512 // 64]]


def put_heads(h, wgs, idx8, t2):
    r = np.arange(h.shape[0])
    page = np.zeros((h.shape[0], t2))
    page[r[:, None], idx8[r % 512 // 64]] = wgs[r // 4 % 128] * h
    return page


T, S, P, T2, K, H, N = 4096, 1024, 1024, 2048, 1024, 1024, 384

def setup_inputs():
    n = np.random.standard_normal
    s = mx_kscale(K)[:, None]
    u = mx_kscale(H)[:, None]
    d = {}
    d["tab_words"], d["tab_scales"] = pack_weight(n((K, T)) * s, "e4m3")
    d["offs"] = striped(np.random.permutation(T)[:S])
    d["offs2"] = striped8(np.stack([np.random.permutation(T2)[:S] for _ in range(8)]))
    d["offs3"] = striped8(np.stack([np.random.permutation(T2)[:P] for _ in range(8)]))
    d["w1"] = (0.42 * n((K, H)) / s / K ** 0.5).astype(np.float32)
    d["b1"] = np.random.uniform(-0.7, 0.7, H).astype(np.float32)
    d["w2_words"], d["w2_scales"] = pack_weight(n((K, H)) / s * u.T / K ** 0.5, "e4m3")
    d["wgs"] = np.repeat(np.random.uniform(0.5, 2.0, (8, S)), 16, axis=0).astype(np.float32)
    d["wgt"] = np.repeat(np.random.uniform(0.5, 2.0, (8, P)), 16, axis=0).astype(np.float32)
    d["lens"] = (n((H, P)) * u).astype(np.float32)
    d["w4_words"], d["w4_scales"] = pack_weight(0.24 * n((H, N)) / u / H ** 0.5, "e2m1")
    d["b4"] = np.random.uniform(-0.7, 0.7, N).astype(np.float32)
    return d

def reference(tab_words, tab_scales, offs, offs2, offs3, w1, b1, w2_words, w2_scales,
              wgs, wgt, lens, w4_words, w4_scales, b4):
    v = unpack_weight(tab_words, tab_scales, "e4m3")[:, unstriped(offs)]
    phase = (mxq(f64(w1), 0, "e4m3").T @ v) + f64(b1)[:, None]
    level = unpack_weight(w2_words, w2_scales, "e4m3").T @ v
    h = np.cos(phase) * level
    page = put_heads(h, f64(wgs), unstriped8(offs2), T2)
    x = heads(page, f64(wgt), unstriped8(offs3))
    z = mxq(x + f64(lens), 0, "e4m3")
    y = unpack_weight(w4_words, w4_scales, "e2m1").T @ z
    return np.sin(y + f64(b4)[:, None])

@@ -1,0 +1,262 @@
+import math
+from contextlib import ExitStack
+
+import concourse.mybir as mybir
+from concourse.masks import make_identity
+
+T, S, M, T2, K, H, N = 4096, 1024, 1024, 2048, 1024, 1024, 384
+FLOPS = 2 * (2 * K * H * S + H * N * M)
+
+F32 = mybir.dt.float32
+BF16 = mybir.dt.bfloat16
+I32 = mybir.dt.int32
+U32 = mybir.dt.uint32
+U16 = mybir.dt.uint16
+U8 = mybir.dt.uint8
+FP8X4 = mybir.dt.float8_e4m3fn_x4
+FP4X4 = mybir.dt.float4_e2m1fn_x4
+ACT = mybir.ActivationFunctionType
+ALU = mybir.AluOpType
+
+P = 128
+KIB = 1024
+FIRST_CUTS = (0, 256, 512, 1024)
+LATER_CUTS = (0, 512, 1024)
+M_CUTS = (0, 256, 512, 768, 896, 1024)
+
+
+def tile_list_dome_projector_blend_kernel(
+    tc, tab_words, tab_scales, offs, offs2, offs3, w1, b1, w2_words, w2_scales,
+    wgs, wgt, lens, w4_words, w4_scales, b4, out,
+):
+    nc = tc.nc
+    with ExitStack() as ctx:
+        lists = ctx.enter_context(tc.tile_pool(name="lists", bufs=1))
+        keep = ctx.enter_context(tc.tile_pool(name="keep", bufs=1))
+        shared = ctx.enter_context(tc.tile_pool(name="shared", bufs=1))
+        ring = ctx.enter_context(tc.tile_pool(name="ring", bufs=2))
+        psum = ctx.enter_context(tc.psum_pool(name="psum", bufs=2))
+
+        def placed(name, shape, dtype, kib):
+            return shared.tile(shape, dtype, name=name, offset=kib * KIB, align_bytes=64)
+
+        pick = lists.tile([P, S // 16], U16, name="pick")
+        put = lists.tile([P, S // 16], U16, name="put")
+        get = lists.tile([P, M // 16], U16, name="get")
+
+        tab = [placed("tab%d" % a, [P, T], U32, 16 * a) for a in range(2)]
+        w1_raw = {(a, b): placed("w1_raw%d%d" % (a, b), [P, 4, 512], F32, 32 + 8 * (2 * b + a))
+                  for a in range(2) for b in range(2)}
+        w2_raw = [placed("w2_raw%d" % b, [P, 2, 512], U32, 80 + 4 * b) for b in range(2)]
+        page_kib = (64, 72, 0, 8, 16, 24, 80, 88)
+
+        tab_sc = placed("tab_sc", [P, T], U8, 96)
+        w2_sc_raw = placed("w2_sc_raw", [P, H], U8, 100)
+        w4_sc = keep.tile([P, 2, N], U8, name="w4_sc", align_bytes=64)
+        w4_codes = keep.tile([P, 2, 2 * N], U8, name="w4_codes", align_bytes=64)
+        wgs_sb = keep.tile([P, S], F32, name="wgs_sb")
+        wgt_sb = keep.tile([P, M], F32, name="wgt_sb")
+        b1_sb = keep.tile([P, 2, 4], F32, name="b1_sb")
+        b4_sb = keep.tile([P, 3], F32, name="b4_sb")
+        b4_shift = keep.tile([P, 3], F32, name="b4_shift")
+        ones = keep.tile([P, 1], F32, name="ones")
+        half_pi = keep.tile([P, 1], F32, name="half_pi")
+        full_pi = keep.tile([P, 1], F32, name="full_pi")
+        neg_half_pi = keep.tile([P, 1], F32, name="neg_half_pi")
+        ident = keep.tile([P, P], F32, name="ident")
+
+        def load_w1(a, b):
+            rows = w1[512 * a:512 * (a + 1), 512 * b:512 * (b + 1)]
+            nc.sync.dma_start(out=w1_raw[(a, b)][:], in_=rows.rearrange("(p j) c -> p j c", j=4))
+
+        def load_w2(b):
+            words = w2_words.rearrange("a p c i -> p a (c i)").bitcast(I32)
+            nc.sync.dma_start(out=w2_raw[b][:].bitcast(I32), in_=words[:, :, 512 * b:512 * (b + 1)])
+
+        nc.vector.memset(tab_sc[:].bitcast(I32), 0)
+        nc.vector.memset(w2_sc_raw[:].bitcast(I32), 0)
+        nc.vector.memset(w4_sc[:].rearrange("p a n -> p (a n)").bitcast(I32), 0)
+        for q in range(4):
+            nc.gpsimd.dma_start(out=tab_sc[32 * q:32 * q + 8, :].bitcast(I32),
+                                in_=tab_scales[:, 4 * q:4 * q + 4, :].bitcast(I32))
+        for q in range(4):
+            nc.gpsimd.dma_start(out=w2_sc_raw[32 * q:32 * q + 8, :].bitcast(I32),
+                                in_=w2_scales[:, 4 * q:4 * q + 4, :].bitcast(I32))
+        nc.gpsimd.dma_start(out=b1_sb[:], in_=b1.rearrange("(b p i) -> p b i", b=2, i=4))
+
+        load_w1(0, 0)
+        load_w1(1, 0)
+        nc.sync.dma_start(pick[:], offs)
+        load_w2(0)
+        for a in range(2):
+            nc.sync.dma_start(out=tab[a][:].bitcast(I32),
+                              in_=tab_words[a].rearrange("p t i -> p (t i)").bitcast(I32))
+        nc.sync.dma_start(put[:], offs2)
+        nc.sync.dma_start(out=wgs_sb[:], in_=wgs)
+        load_w1(0, 1)
+        load_w1(1, 1)
+        load_w2(1)
+        nc.sync.dma_start(get[:], offs3)
+        nc.sync.dma_start(out=wgt_sb[:], in_=wgt)
+        nc.sync.dma_start(out=w4_codes[:].bitcast(I32), in_=w4_words.rearrange("a p n -> p a n").bitcast(I32))
+        for q in range(4):
+            nc.sync.dma_start(out=w4_sc[32 * q:32 * q + 4, :, :].bitcast(I32),
+                              in_=w4_scales[:, 4 * q:4 * q + 4, :].rearrange("a r n -> r a n").bitcast(I32))
+        with nc.allow_non_contiguous_dma(reason="one bias value a partition"):
+            nc.sync.dma_start(out=b4_sb[:], in_=b4.rearrange("(t p) -> p t", p=P))
+
+        nc.gpsimd.memset(ones[:], 1.0)
+        for const, value in ((half_pi, math.pi / 2), (full_pi, math.pi), (neg_half_pi, -math.pi / 2)):
+            nc.gpsimd.tensor_scalar(const[:], ones[:], value, 0.0, ALU.mult, ALU.add)
+        make_identity(nc, ident[:])
+        nc.gpsimd.tensor_scalar(b4_shift[:], b4_sb[:], 1.0, -math.pi / 2, ALU.mult, ALU.add)
+
+        pages = []
+
+        def new_page(engine):
+            page = placed("page%d" % len(pages), [P, T2], F32, page_kib[len(pages)])
+            engine.memset(page[:], 0.0)
+            pages.append(page)
+
+        new_page(nc.vector)
+        new_page(nc.vector)
+
+        w1_codes = keep.tile([P, 2, H], U32, name="w1_codes", align_bytes=64)
+        w1_sc = keep.tile([P, 2, H], U8, name="w1_sc", align_bytes=64)
+        w2_codes = keep.tile([P, 2, H], U32, name="w2_codes", align_bytes=64)
+        w2_sc = keep.tile([P, H], U8, name="w2_sc", align_bytes=64)
+
+        def prepare_w1(a, b):
+            grouped = shared.tile([P, 2048], BF16, name="w1_grouped%d%d" % (a, b), offset=(88 + 4 * a) * KIB,
+                                  align_bytes=64)
+            nc.scalar.copy(out=grouped[:].rearrange("p (i m j) -> p m j i", i=4, j=4),
+                           in_=w1_raw[(a, b)][:].rearrange("p j (m i) -> p m j i", i=4))
+            cols = slice(512 * b, 512 * (b + 1))
+            nc.vector.quantize_mx(out=w1_codes[:, a, cols].bitcast(FP8X4), scales=w1_sc[:, a, cols], in_=grouped[:])
+
+        def prepare_w2(b, copy):
+            for a in range(2):
+                copy(out=w2_codes[:, a, 512 * b:512 * (b + 1)].rearrange("p (i m) -> p m i", i=4),
+                     in_=w2_raw[b][:, a, :].rearrange("p (m i) -> p m i", i=4))
+
+        prepare_w1(0, 0)
+        prepare_w1(1, 0)
+        v_sc = keep.tile([P, S], U8, name="v_sc", align_bytes=64)
+        nc.vector.tensor_copy(v_sc[:], tab_sc[:].indirect(pick[:]))
+        nc.vector.tensor_copy(out=w2_sc[:].rearrange("p (b i m) -> p b i m", b=2, i=4),
+                              in_=w2_sc_raw[:].rearrange("p (b m i) -> p b i m", b=2, i=4))
+        prepare_w2(0, nc.vector.tensor_copy)
+        v_codes = [placed("v_codes0", [P, S], U32, 97), keep.tile([P, S], U32, name="v_codes1", align_bytes=64)]
+        nc.vector.tensor_copy(v_codes[0][:], tab[0][:].indirect(pick[:]))
+        for lo, hi in zip(FIRST_CUTS, FIRST_CUTS[1:]):
+            nc.vector.tensor_copy(v_codes[1][:, lo:hi], tab[1][:].indirect(pick[:, lo // 16:hi // 16]))
+
+        lens_sb = {}
+
+        def load_lens(b):
+            rows = lens[512 * b:512 * (b + 1), :].rearrange("(p i) m -> p i m", i=4)
+            for u in range(2):
+                pair = placed("lens%d%d" % (b, u), [P, 2, M], F32, 32 + 8 * (2 * b + u))
+                nc.sync.dma_start(out=pair[:], in_=rows[:, 2 * u:2 * u + 2, :])
+                lens_sb[(b, u)] = pair
+
+        def first_stage(t):
+            b, i = divmod(t, 4)
+            cuts = FIRST_CUTS if t == 0 else LATER_CUTS
+            rows = slice(P * t, P * (t + 1))
+            h = ring.tile([P, S], F32, name="h", bufs=3)
+            for lo, hi in zip(cuts, cuts[1:]):
+                cols = slice(lo, hi)
+                width = hi - lo
+                phase = psum.tile([P, 512], F32, name="bank_a")
+                level = psum.tile([P, 512], F32, name="bank_b")
+                for a in range(2):
+                    nc.tensor.matmul_mx(out=phase[:, :width], lhsT=w1_codes[:, a, rows].bitcast(FP8X4),
+                                        lhsT_scale=w1_sc[:, a, rows], rhs=v_codes[a][:, cols].bitcast(FP8X4),
+                                        rhs_scale=v_sc[4 * a:P, cols], start=(a == 0), stop=(a == 1))
+                for a in range(2):
+                    nc.tensor.matmul_mx(out=level[:, :width], lhsT=w2_codes[:, a, rows].bitcast(FP8X4),
+                                        lhsT_scale=w2_sc[4 * a:P, rows], rhs=v_codes[a][:, cols].bitcast(FP8X4),
+                                        rhs_scale=v_sc[4 * a:P, cols], start=(a == 0), stop=(a == 1))
+                size = ring.tile([P, 512], F32, name="size")
+                cosine = ring.tile([P, 512], F32, name="cosine", bufs=3)
+                nc.scalar.activation(size[:, :width], phase[:, :width], ACT.Abs, bias=b1_sb[:, b, i:i + 1])
+                nc.scalar.activation(cosine[:, :width], size[:, :width], ACT.Sin, bias=half_pi[:], scale=-1.0)
+                nc.vector.tensor_tensor(h[:, cols], level[:, :width], cosine[:, :width], ALU.mult)
+                if t == 0:
+                    nc.vector.tensor_tensor(pages[t][:].indirect(put[:, lo // 16:hi // 16]), h[:, cols],
+                                            wgs_sb[:, cols], ALU.mult)
+            if t > 0:
+                nc.vector.tensor_tensor(pages[t][:].indirect(put[:]), h[:], wgs_sb[:], ALU.mult)
+
+        first_stage(0)
+        for t in range(2, 6):
+            new_page(nc.gpsimd)
+        first_stage(1)
+        load_lens(0)
+        prepare_w1(0, 1)
+        prepare_w1(1, 1)
+        prepare_w2(1, nc.scalar.copy)
+        load_lens(1)
+        new_page(nc.gpsimd)
+        new_page(nc.gpsimd)
+        for t in range(2, 8):
+            first_stage(t)
+
+        def make_z(b, lo, hi):
+            width = hi - lo
+            tiles = width // P
+            words = psum.tile([P, 512], F32, name="bank_d")
+            for u in range(2):
+                x = []
+                for e in range(2):
+                    picked = ring.tile([P, 256], F32, name="picked", bufs=4)
+                    nc.vector.tensor_tensor(picked[:, :width],
+                                            pages[4 * b + 2 * u + e][:].indirect(get[:, lo // 16:hi // 16]),
+                                            wgt_sb[:, lo:hi], ALU.mult)
+                    x.append(picked)
+                turned = psum.tile([P, 512], F32, name="bank_c")
+                places = [(mt, e) for e in range(2) for mt in range(tiles)]
+                for n, (mt, e) in enumerate(places):
+                    col = P * (2 * mt + e)
+                    nc.tensor.matmul(turned[:, col:col + P], lhsT=lens_sb[(b, u)][:, e, lo + P * mt:lo + P * (mt + 1)],
+                                     rhs=ident[:], start=(n == 0), stop=False, is_transpose=True)
+                for n, (mt, e) in enumerate(places):
+                    col = P * (2 * mt + e)
+                    nc.tensor.matmul(turned[:, col:col + P], lhsT=x[e][:, P * mt:P * (mt + 1)],
+                                     rhs=ident[:], start=False, stop=(n == len(places) - 1), is_transpose=True)
+                pairs = ring.tile([P, 512], BF16, name="pairs")
+                nc.scalar.copy(out=pairs[:, :2 * width].rearrange("m (t p e) -> m t p e", e=2, p=P),
+                               in_=turned[:, :2 * width].rearrange("m (t e p) -> m t p e", e=2, p=P))
+                for mt in range(tiles):
+                    col = width * u + P * mt
+                    nc.tensor.transpose(words[:, col:col + P], pairs[:].bitcast(F32)[:, P * mt:P * (mt + 1)], ident[:])
+            z = ring.tile([P, 1024], BF16, name="z", align_bytes=64)
+            nc.scalar.copy(out=z[:].bitcast(F32)[:, :2 * width].rearrange("p (m u) -> p m u", u=2),
+                           in_=words[:, :2 * width].rearrange("p (u m) -> p m u", u=2))
+            z_codes = ring.tile([P, 256], U32, name="z_codes", bufs=4, align_bytes=64)
+            z_sc = ring.tile([P, 256], U8, name="z_sc", bufs=4, align_bytes=64)
+            nc.vector.quantize_mx(out=z_codes[:, :width].bitcast(FP8X4), scales=z_sc[:, :width], in_=z[:, :4 * width])
+            return z_codes, z_sc
+
+        for lo, hi in zip(M_CUTS, M_CUTS[1:]):
+            width = hi - lo
+            z_parts = [make_z(b, lo, hi) for b in range(2)]
+            bank_01 = psum.tile([P, 512], F32, name="bank_a")
+            bank_2 = psum.tile([P, 512], F32, name="bank_b")
+            sums = [bank_01[:, :width], bank_01[:, 256:256 + width], bank_2[:, :width]]
+            folded = ring.tile([P, 3, 256], F32, name="folded")
+            for nt in range(3):
+                for b in (1, 0):
+                    z_codes, z_sc = z_parts[b]
+                    nc.tensor.matmul_mx(out=sums[nt], lhsT=w4_codes[:, b, 256 * nt:256 * (nt + 1)].bitcast(FP4X4),
+                                        lhsT_scale=w4_sc[:, b, P * nt:P * (nt + 1)],
+                                        rhs=z_codes[:, :width].bitcast(FP8X4), rhs_scale=z_sc[:, :width],
+                                        start=(b == 1), stop=(b == 0))
+            for nt in range(3):
+                nc.scalar.activation(folded[:, nt, :width], sums[nt], ACT.Abs, bias=b4_shift[:, nt:nt + 1])
+            twice = ring.tile([P, 3, 256], F32, name="twice")
+            nc.scalar.activation(twice[:, :, :width], folded[:, :, :width], ACT.Abs, bias=full_pi[:], scale=-1.0)
+            result = ring.tile([P, 3, 256], F32, name="result")
+            nc.scalar.activation(result[:, :, :width], twice[:, :, :width], ACT.Sin, bias=neg_half_pi[:])
+            nc.sync.dma_start(out=out[:, lo:hi].rearrange("(t p) m -> p t m", p=P), in_=result[:, :, :width])

@@ -48,7 +48,7 @@ def tile_list_dome_projector_blend_kernel(
         w1_raw = {(a, b): placed("w1_raw%d%d" % (a, b), [P, 4, 512], F32, 32 + 8 * (2 * b + a))
                   for a in range(2) for b in range(2)}
         w2_raw = [placed("w2_raw%d" % b, [P, 2, 512], U32, 80 + 4 * b) for b in range(2)]
-        page_kib = (64, 72, 0, 8, 16, 24, 80, 88)
+        pages = [placed("page%d" % n, [P, T2], F32, 64 + 8 * n) for n in range(2)]
 
         tab_sc = placed("tab_sc", [P, T], U8, 96)
         w2_sc_raw = placed("w2_sc_raw", [P, H], U8, 100)
@@ -61,8 +61,6 @@ def tile_list_dome_projector_blend_kernel(
         b4_shift = keep.tile([P, 3], F32, name="b4_shift")
         ones = keep.tile([P, 1], F32, name="ones")
         half_pi = keep.tile([P, 1], F32, name="half_pi")
-        full_pi = keep.tile([P, 1], F32, name="full_pi")
-        neg_half_pi = keep.tile([P, 1], F32, name="neg_half_pi")
         ident = keep.tile([P, P], F32, name="ident")
 
         def load_w1(a, b):
@@ -76,21 +74,23 @@ def tile_list_dome_projector_blend_kernel(
         nc.vector.memset(tab_sc[:].bitcast(I32), 0)
         nc.vector.memset(w2_sc_raw[:].bitcast(I32), 0)
         nc.vector.memset(w4_sc[:].rearrange("p a n -> p (a n)").bitcast(I32), 0)
-        for q in range(4):
-            nc.gpsimd.dma_start(out=tab_sc[32 * q:32 * q + 8, :].bitcast(I32),
-                                in_=tab_scales[:, 4 * q:4 * q + 4, :].bitcast(I32))
-        for q in range(4):
-            nc.gpsimd.dma_start(out=w2_sc_raw[32 * q:32 * q + 8, :].bitcast(I32),
-                                in_=w2_scales[:, 4 * q:4 * q + 4, :].bitcast(I32))
-        nc.gpsimd.dma_start(out=b1_sb[:], in_=b1.rearrange("(b p i) -> p b i", b=2, i=4))
+        def load_tab(a):
+            nc.sync.dma_start(out=tab[a][:].bitcast(I32),
+                              in_=tab_words[a].rearrange("p t i -> p (t i)").bitcast(I32))
 
         load_w1(0, 0)
         load_w1(1, 0)
+        for q in range(4):
+            nc.sync.dma_start(out=tab_sc[32 * q:32 * q + 8, :].bitcast(I32),
+                              in_=tab_scales[:, 4 * q:4 * q + 4, :].bitcast(I32))
         nc.sync.dma_start(pick[:], offs)
+        load_tab(0)
+        for q in range(4):
+            nc.sync.dma_start(out=w2_sc_raw[32 * q:32 * q + 8, :].bitcast(I32),
+                              in_=w2_scales[:, 4 * q:4 * q + 4, :].bitcast(I32))
+        load_tab(1)
         load_w2(0)
-        for a in range(2):
-            nc.sync.dma_start(out=tab[a][:].bitcast(I32),
-                              in_=tab_words[a].rearrange("p t i -> p (t i)").bitcast(I32))
+        nc.sync.dma_start(out=b1_sb[:], in_=b1.rearrange("(b p i) -> p b i", b=2, i=4))
         nc.sync.dma_start(put[:], offs2)
         nc.sync.dma_start(out=wgs_sb[:], in_=wgs)
         load_w1(0, 1)
@@ -106,51 +106,44 @@ def tile_list_dome_projector_blend_kernel(
             nc.sync.dma_start(out=b4_sb[:], in_=b4.rearrange("(t p) -> p t", p=P))
 
         nc.gpsimd.memset(ones[:], 1.0)
-        for const, value in ((half_pi, math.pi / 2), (full_pi, math.pi), (neg_half_pi, -math.pi / 2)):
-            nc.gpsimd.tensor_scalar(const[:], ones[:], value, 0.0, ALU.mult, ALU.add)
+        nc.gpsimd.tensor_scalar(half_pi[:], ones[:], math.pi / 2, 0.0, ALU.mult, ALU.add)
         make_identity(nc, ident[:])
-        nc.gpsimd.tensor_scalar(b4_shift[:], b4_sb[:], 1.0, -math.pi / 2, ALU.mult, ALU.add)
+        for page in pages:
+            nc.vector.memset(page[:], 0.0)
 
-        pages = []
-
-        def new_page(engine):
-            page = placed("page%d" % len(pages), [P, T2], F32, page_kib[len(pages)])
-            engine.memset(page[:], 0.0)
-            pages.append(page)
-
-        new_page(nc.vector)
-        new_page(nc.vector)
-
-        w1_codes = keep.tile([P, 2, H], U32, name="w1_codes", align_bytes=64)
-        w1_sc = keep.tile([P, 2, H], U8, name="w1_sc", align_bytes=64)
-        w2_codes = keep.tile([P, 2, H], U32, name="w2_codes", align_bytes=64)
+        w1_codes = {}
+        w1_sc = keep.tile([P, 8, 2 * P], U8, name="w1_sc", align_bytes=64)
+        w2_codes = keep.tile([P, 8, 2 * P], U32, name="w2_codes", align_bytes=64)
         w2_sc = keep.tile([P, H], U8, name="w2_sc", align_bytes=64)
 
-        def prepare_w1(a, b):
-            grouped = shared.tile([P, 2048], BF16, name="w1_grouped%d%d" % (a, b), offset=(88 + 4 * a) * KIB,
-                                  align_bytes=64)
-            nc.scalar.copy(out=grouped[:].rearrange("p (i m j) -> p m j i", i=4, j=4),
-                           in_=w1_raw[(a, b)][:].rearrange("p j (m i) -> p m j i", i=4))
-            cols = slice(512 * b, 512 * (b + 1))
-            nc.vector.quantize_mx(out=w1_codes[:, a, cols].bitcast(FP8X4), scales=w1_sc[:, a, cols], in_=grouped[:])
-
-        def prepare_w2(b, copy):
+        def prepare_w1(t):
+            b, i = divmod(t, 4)
+            grouped = ring.tile([P, 2, 512], BF16, name="w1_grouped", bufs=3, align_bytes=64)
+            w1_codes[t] = placed("w1_codes%d" % t, [P, 2 * P], U32, 136 + t if t < 2 else 16 + t)
             for a in range(2):
-                copy(out=w2_codes[:, a, 512 * b:512 * (b + 1)].rearrange("p (i m) -> p m i", i=4),
-                     in_=w2_raw[b][:, a, :].rearrange("p (m i) -> p m i", i=4))
+                nc.scalar.copy(out=grouped[:, a, :].rearrange("p (m j) -> p m j", j=4),
+                               in_=w1_raw[(a, b)][:].rearrange("p j (m i) -> p i m j", i=4)[:, i])
+            nc.vector.quantize_mx(out=w1_codes[t][:].bitcast(FP8X4), scales=w1_sc[:, t, :],
+                                  in_=grouped[:].rearrange("p a c -> p (a c)"))
 
-        prepare_w1(0, 0)
-        prepare_w1(1, 0)
+        def prepare_w2(t):
+            b, i = divmod(t, 4)
+            nc.scalar.copy(out=w2_codes[:, t, :].rearrange("p (a m) -> p a m", a=2),
+                           in_=w2_raw[b][:].rearrange("p a (m i) -> p i a m", i=4)[:, i])
+
+        prepare_w1(0)
+        prepare_w1(1)
         v_sc = keep.tile([P, S], U8, name="v_sc", align_bytes=64)
         nc.vector.tensor_copy(v_sc[:], tab_sc[:].indirect(pick[:]))
+        v_codes = [placed("v_codes0", [P, S], U32, 96), placed("v_codes1", [P, S], U32, 100)]
+        nc.vector.tensor_copy(v_codes[0][:], tab[0][:].indirect(pick[:]))
         nc.vector.tensor_copy(out=w2_sc[:].rearrange("p (b i m) -> p b i m", b=2, i=4),
                               in_=w2_sc_raw[:].rearrange("p (b m i) -> p b i m", b=2, i=4))
-        prepare_w2(0, nc.vector.tensor_copy)
-        v_codes = [placed("v_codes0", [P, S], U32, 97), keep.tile([P, S], U32, name="v_codes1", align_bytes=64)]
-        nc.vector.tensor_copy(v_codes[0][:], tab[0][:].indirect(pick[:]))
         for lo, hi in zip(FIRST_CUTS, FIRST_CUTS[1:]):
             nc.vector.tensor_copy(v_codes[1][:, lo:hi], tab[1][:].indirect(pick[:, lo // 16:hi // 16]))
 
+        prepare_w1(2)
+        prepare_w1(3)
         lens_sb = {}
 
         def load_lens(b):
@@ -160,103 +153,144 @@ def tile_list_dome_projector_blend_kernel(
                 nc.sync.dma_start(out=pair[:], in_=rows[:, 2 * u:2 * u + 2, :])
                 lens_sb[(b, u)] = pair
 
-        def first_stage(t):
+        ARENA = 104
+
+        def scatter(t, h, lo, hi):
+            nc.vector.tensor_tensor(pages[t % 2][:].indirect(put[:, lo // 16:hi // 16]), h[:, lo:hi],
+                                    wgs_sb[:, lo:hi], ALU.mult)
+
+        def make_h(t):
             b, i = divmod(t, 4)
             cuts = FIRST_CUTS if t == 0 else LATER_CUTS
             rows = slice(P * t, P * (t + 1))
+            prepare_w2(t)
             h = ring.tile([P, S], F32, name="h", bufs=3)
+            cosines = [placed("cosine%d%d" % (t, n), [P, 512], F32, ARENA + 4 * t + 2 * n) for n in range(2)]
             for lo, hi in zip(cuts, cuts[1:]):
                 cols = slice(lo, hi)
                 width = hi - lo
                 phase = psum.tile([P, 512], F32, name="bank_a")
                 level = psum.tile([P, 512], F32, name="bank_b")
                 for a in range(2):
-                    nc.tensor.matmul_mx(out=phase[:, :width], lhsT=w1_codes[:, a, rows].bitcast(FP8X4),
-                                        lhsT_scale=w1_sc[:, a, rows], rhs=v_codes[a][:, cols].bitcast(FP8X4),
+                    nc.tensor.matmul_mx(out=phase[:, :width], lhsT=w1_codes[t][:, P * a:P * (a + 1)].bitcast(FP8X4),
+                                        lhsT_scale=w1_sc[:, t, P * a:P * (a + 1)], rhs=v_codes[a][:, cols].bitcast(FP8X4),
                                         rhs_scale=v_sc[4 * a:P, cols], start=(a == 0), stop=(a == 1))
                 for a in range(2):
-                    nc.tensor.matmul_mx(out=level[:, :width], lhsT=w2_codes[:, a, rows].bitcast(FP8X4),
+                    nc.tensor.matmul_mx(out=level[:, :width], lhsT=w2_codes[:, t, P * a:P * (a + 1)].bitcast(FP8X4),
                                         lhsT_scale=w2_sc[4 * a:P, rows], rhs=v_codes[a][:, cols].bitcast(FP8X4),
                                         rhs_scale=v_sc[4 * a:P, cols], start=(a == 0), stop=(a == 1))
                 size = ring.tile([P, 512], F32, name="size")
-                cosine = ring.tile([P, 512], F32, name="cosine", bufs=3)
+                cosine = cosines[lo // 512][:, lo % 512:lo % 512 + width]
                 nc.scalar.activation(size[:, :width], phase[:, :width], ACT.Abs, bias=b1_sb[:, b, i:i + 1])
-                nc.scalar.activation(cosine[:, :width], size[:, :width], ACT.Sin, bias=half_pi[:], scale=-1.0)
-                nc.vector.tensor_tensor(h[:, cols], level[:, :width], cosine[:, :width], ALU.mult)
+                nc.scalar.activation(cosine, size[:, :width], ACT.Sin, bias=half_pi[:], scale=-1.0)
+                nc.vector.tensor_tensor(h[:, cols], level[:, :width], cosine, ALU.mult)
                 if t == 0:
-                    nc.vector.tensor_tensor(pages[t][:].indirect(put[:, lo // 16:hi // 16]), h[:, cols],
-                                            wgs_sb[:, cols], ALU.mult)
-            if t > 0:
-                nc.vector.tensor_tensor(pages[t][:].indirect(put[:]), h[:], wgs_sb[:], ALU.mult)
+                    scatter(0, h, lo, hi)
+            return h
 
-        first_stage(0)
-        for t in range(2, 6):
-            new_page(nc.gpsimd)
-        first_stage(1)
-        load_lens(0)
-        prepare_w1(0, 1)
-        prepare_w1(1, 1)
-        prepare_w2(1, nc.scalar.copy)
-        load_lens(1)
-        new_page(nc.gpsimd)
-        new_page(nc.gpsimd)
-        for t in range(2, 8):
-            first_stage(t)
+        def gather(t, x, lo, hi):
+            nc.vector.tensor_tensor(x, pages[t % 2][:].indirect(get[:, lo // 16:hi // 16]), wgt_sb[:, lo:hi], ALU.mult)
 
-        def make_z(b, lo, hi):
-            width = hi - lo
-            tiles = width // P
+        def add_lens(b, u, x, lo):
+            turned = psum.tile([P, 512], F32, name="bank_c")
+            steps = [(lens_sb[(b, u)][:, e, :], e) for e in range(2)] + [(x[e][:], e) for e in range(2)]
+            steps = [(rows, e, mt) for rows, e in steps for mt in range(2)]
+            for n, (rows, e, mt) in enumerate(steps):
+                col = P * (2 * mt + e)
+                nc.tensor.matmul(turned[:, col:col + P], lhsT=rows[:, lo + P * mt:lo + P * (mt + 1)], rhs=ident[:],
+                                 start=(n == 0), stop=(n == len(steps) - 1), is_transpose=True)
+            pairs = ring.tile([P, 512], BF16, name="pairs", bufs=6)
+            nc.scalar.copy(out=pairs[:].rearrange("m (t p e) -> m t p e", e=2, p=P),
+                           in_=turned[:].rearrange("m (t e p) -> m t p e", e=2, p=P))
+            return pairs
+
+        def turn_back(sources):
             words = psum.tile([P, 512], F32, name="bank_d")
-            for u in range(2):
-                x = []
-                for e in range(2):
-                    picked = ring.tile([P, 256], F32, name="picked", bufs=4)
-                    nc.vector.tensor_tensor(picked[:, :width],
-                                            pages[4 * b + 2 * u + e][:].indirect(get[:, lo // 16:hi // 16]),
-                                            wgt_sb[:, lo:hi], ALU.mult)
-                    x.append(picked)
-                turned = psum.tile([P, 512], F32, name="bank_c")
-                places = [(mt, e) for e in range(2) for mt in range(tiles)]
-                for n, (mt, e) in enumerate(places):
-                    col = P * (2 * mt + e)
-                    nc.tensor.matmul(turned[:, col:col + P], lhsT=lens_sb[(b, u)][:, e, lo + P * mt:lo + P * (mt + 1)],
-                                     rhs=ident[:], start=(n == 0), stop=False, is_transpose=True)
-                for n, (mt, e) in enumerate(places):
-                    col = P * (2 * mt + e)
-                    nc.tensor.matmul(turned[:, col:col + P], lhsT=x[e][:, P * mt:P * (mt + 1)],
-                                     rhs=ident[:], start=False, stop=(n == len(places) - 1), is_transpose=True)
-                pairs = ring.tile([P, 512], BF16, name="pairs")
-                nc.scalar.copy(out=pairs[:, :2 * width].rearrange("m (t p e) -> m t p e", e=2, p=P),
-                               in_=turned[:, :2 * width].rearrange("m (t e p) -> m t p e", e=2, p=P))
-                for mt in range(tiles):
-                    col = width * u + P * mt
-                    nc.tensor.transpose(words[:, col:col + P], pairs[:].bitcast(F32)[:, P * mt:P * (mt + 1)], ident[:])
-            z = ring.tile([P, 1024], BF16, name="z", align_bytes=64)
-            nc.scalar.copy(out=z[:].bitcast(F32)[:, :2 * width].rearrange("p (m u) -> p m u", u=2),
-                           in_=words[:, :2 * width].rearrange("p (u m) -> p m u", u=2))
-            z_codes = ring.tile([P, 256], U32, name="z_codes", bufs=4, align_bytes=64)
-            z_sc = ring.tile([P, 256], U8, name="z_sc", bufs=4, align_bytes=64)
-            nc.vector.quantize_mx(out=z_codes[:, :width].bitcast(FP8X4), scales=z_sc[:, :width], in_=z[:, :4 * width])
-            return z_codes, z_sc
+            for n, (pairs, mt) in enumerate((pairs, mt) for pairs in sources for mt in range(2)):
+                nc.tensor.transpose(words[:, P * n:P * (n + 1)], pairs[:].bitcast(F32)[:, P * mt:P * (mt + 1)],
+                                    ident[:])
+            return words
 
-        for lo, hi in zip(M_CUTS, M_CUTS[1:]):
+        def quantise_z(b, z, lo, hi):
+            nc.vector.quantize_mx(out=z_codes[b][:, lo:hi].bitcast(FP8X4), scales=z_sc[b][:, lo:hi],
+                                  in_=z[:, :4 * (hi - lo)])
+
+        def last_product(lo, hi, tags):
             width = hi - lo
-            z_parts = [make_z(b, lo, hi) for b in range(2)]
-            bank_01 = psum.tile([P, 512], F32, name="bank_a")
-            bank_2 = psum.tile([P, 512], F32, name="bank_b")
-            sums = [bank_01[:, :width], bank_01[:, 256:256 + width], bank_2[:, :width]]
-            folded = ring.tile([P, 3, 256], F32, name="folded")
-            for nt in range(3):
-                for b in (1, 0):
-                    z_codes, z_sc = z_parts[b]
-                    nc.tensor.matmul_mx(out=sums[nt], lhsT=w4_codes[:, b, 256 * nt:256 * (nt + 1)].bitcast(FP4X4),
+            banks = [psum.tile([P, 512], F32, name=tag) for tag in tags]
+            per_bank = 512 // width
+            for b in range(2):
+                for nt in range(3):
+                    col = width * (nt % per_bank)
+                    nc.tensor.matmul_mx(out=banks[nt // per_bank][:, col:col + width],
+                                        lhsT=w4_codes[:, b, 256 * nt:256 * (nt + 1)].bitcast(FP4X4),
                                         lhsT_scale=w4_sc[:, b, P * nt:P * (nt + 1)],
-                                        rhs=z_codes[:, :width].bitcast(FP8X4), rhs_scale=z_sc[:, :width],
-                                        start=(b == 1), stop=(b == 0))
+                                        rhs=z_codes[b][:, lo:hi].bitcast(FP8X4), rhs_scale=z_sc[b][:, lo:hi],
+                                        start=(b == 0 and nt % per_bank == 0),
+                                        stop=(b == 1 and (nt == 2 or nt % per_bank == per_bank - 1)))
+            half = ring.tile([P, 3 * 256], F32, name="half")
             for nt in range(3):
-                nc.scalar.activation(folded[:, nt, :width], sums[nt], ACT.Abs, bias=b4_shift[:, nt:nt + 1])
-            twice = ring.tile([P, 3, 256], F32, name="twice")
-            nc.scalar.activation(twice[:, :, :width], folded[:, :, :width], ACT.Abs, bias=full_pi[:], scale=-1.0)
-            result = ring.tile([P, 3, 256], F32, name="result")
-            nc.scalar.activation(result[:, :, :width], twice[:, :, :width], ACT.Sin, bias=neg_half_pi[:])
-            nc.sync.dma_start(out=out[:, lo:hi].rearrange("(t p) m -> p t m", p=P), in_=result[:, :, :width])
+                col = width * (nt % per_bank)
+                nc.scalar.activation(half[:, width * nt:width * (nt + 1)], banks[nt // per_bank][:, col:col + width],
+                                     ACT.Sin, bias=b4_shift[:, nt:nt + 1], scale=0.5)
+            square = ring.tile([P, 3 * 256], F32, name="square")
+            nc.scalar.activation(square[:, :3 * width], half[:, :3 * width], ACT.Square)
+            result = ring.tile([P, 3 * 256], F32, name="result", bufs=3)
+            nc.vector.tensor_scalar(result[:, :3 * width], square[:, :3 * width], -2.0, 1.0, ALU.mult, ALU.add)
+            nc.sync.dma_start(out=out[:, lo:hi].rearrange("(t p) m -> p t m", p=P),
+                              in_=result[:, :3 * width].rearrange("p (t m) -> p t m", t=3))
+
+        z_codes = [keep.tile([P, M], U32, name="z_codes%d" % b, align_bytes=64) for b in range(2)]
+        z_sc = [keep.tile([P, M], U8, name="z_sc%d" % b, align_bytes=64) for b in range(2)]
+        chunks = list(zip(M_CUTS, M_CUTS[1:]))
+        last_words = [keep.tile([P, 2, hi - lo], F32, name="last_words%d" % lo, align_bytes=64) for lo, hi in chunks]
+        x = {}
+        first_pairs = {}
+        make_h(0)
+        load_lens(0)
+        for t in range(1, 8):
+            h = make_h(t)
+            if t == 1:
+                nc.vector.tensor_scalar(b4_shift[:], b4_sb[:], 0.5, -math.pi / 4, ALU.mult, ALU.add)
+            if t in (1, 2):
+                prepare_w1(2 * t + 2)
+                prepare_w1(2 * t + 3)
+            if t == 2:
+                load_lens(1)
+            done = t - 2
+            if done >= 0:
+                x[done % 2] = placed("x%d" % done, [P, M], F32, ARENA + 4 * done + 6)
+                gather(done, x[done % 2][:], 0, M)
+            scatter(t, h, 0, S)
+            if done in (1, 3, 5):
+                b, u = done // 4, done // 2 % 2
+                for lo in range(0, M, 256):
+                    pairs = add_lens(b, u, x, lo)
+                    if u == 0:
+                        first_pairs[lo] = pairs
+                    if done == 3:
+                        words = turn_back((first_pairs[lo], pairs))
+                        z = ring.tile([P, 1024], BF16, name="z", align_bytes=64)
+                        nc.scalar.copy(out=z[:].bitcast(F32).rearrange("p (m u) -> p m u", u=2),
+                                       in_=words[:].rearrange("p (u m) -> p m u", u=2))
+                        quantise_z(0, z, lo, lo + 256)
+                    if done == 5 and lo % 512 == 256:
+                        words = turn_back((first_pairs[lo - 256], pairs))
+                        for (start, end), target in zip(chunks, last_words):
+                            if start // 512 == lo // 512:
+                                nc.scalar.copy(out=target[:, 0, :], in_=words[:, start % 512:start % 512 + end - start])
+
+        bank_tags = (("bank_a", "bank_b"), ("bank_a", "bank_b"), ("bank_c", "bank_c"), ("bank_d",), ("bank_d",))
+        for c, (lo, hi) in enumerate(chunks):
+            width = hi - lo
+            x_pair = placed("x_pair%d" % c, [P, 2, 256], F32, ARENA + 2 * (c % 4))
+            for e in range(2):
+                gather(6 + e, x_pair[:, e, :width], lo, hi)
+            nc.vector.tensor_tensor(last_words[c][:, 1, :].bitcast(BF16).rearrange("p (m e) -> p m e", e=2),
+                                    x_pair[:, :, :width].rearrange("p e m -> p m e"),
+                                    lens_sb[(1, 1)][:, :, lo:hi].rearrange("p e m -> p m e"), ALU.add)
+            z = placed("z_last%d" % c, [P, 1024], BF16, ARENA + 2 * ((c + 2) % 4))
+            nc.scalar.copy(out=z[:].bitcast(F32)[:, :2 * width].rearrange("p (m u) -> p m u", u=2),
+                           in_=last_words[c][:].rearrange("p u m -> p m u"))
+            quantise_z(1, z, lo, hi)
+            last_product(lo, hi, bank_tags[c])

@@ -48,7 +48,7 @@ def tile_list_dome_projector_blend_kernel(
         w1_raw = {(a, b): placed("w1_raw%d%d" % (a, b), [P, 4, 512], F32, 32 + 8 * (2 * b + a))
                   for a in range(2) for b in range(2)}
         w2_raw = [placed("w2_raw%d" % b, [P, 2, 512], U32, 80 + 4 * b) for b in range(2)]
-        pages = [placed("page%d" % n, [P, T2], F32, 64 + 8 * n) for n in range(2)]
+        pages = [placed("page%d" % n, [P, T2], F32, kib) for n, kib in enumerate((64, 72, 88))]
 
         tab_sc = placed("tab_sc", [P, T], U8, 96)
         w2_sc_raw = placed("w2_sc_raw", [P, H], U8, 100)
@@ -113,7 +113,7 @@ def tile_list_dome_projector_blend_kernel(
 
         w1_codes = {}
         w1_sc = keep.tile([P, 8, 2 * P], U8, name="w1_sc", align_bytes=64)
-        w2_codes = keep.tile([P, 8, 2 * P], U32, name="w2_codes", align_bytes=64)
+        w2_codes = placed("w2_codes", [P, 8, 2 * P], U32, 0)
         w2_sc = keep.tile([P, H], U8, name="w2_sc", align_bytes=64)
 
         def prepare_w1(t):
@@ -155,41 +155,64 @@ def tile_list_dome_projector_blend_kernel(
 
         ARENA = 104
 
-        def scatter(t, h, lo, hi):
-            nc.vector.tensor_tensor(pages[t % 2][:].indirect(put[:, lo // 16:hi // 16]), h[:, lo:hi],
-                                    wgs_sb[:, lo:hi], ALU.mult)
+        def products(t, lo, hi):
+            cols = slice(lo, hi)
+            width = hi - lo
+            phase = psum.tile([P, 512], F32, name="bank_a")
+            level = psum.tile([P, 512], F32, name="bank_b")
+            for a in range(2):
+                nc.tensor.matmul_mx(out=phase[:, :width], lhsT=w1_codes[t][:, P * a:P * (a + 1)].bitcast(FP8X4),
+                                    lhsT_scale=w1_sc[:, t, P * a:P * (a + 1)],
+                                    rhs=v_codes[a][:, cols].bitcast(FP8X4),
+                                    rhs_scale=v_sc[4 * a:P, cols], start=(a == 0), stop=(a == 1))
+            for a in range(2):
+                nc.tensor.matmul_mx(out=level[:, :width], lhsT=w2_codes[:, t, P * a:P * (a + 1)].bitcast(FP8X4),
+                                    lhsT_scale=w2_sc[4 * a:P, P * t:P * (t + 1)],
+                                    rhs=v_codes[a][:, cols].bitcast(FP8X4),
+                                    rhs_scale=v_sc[4 * a:P, cols], start=(a == 0), stop=(a == 1))
+            return phase[:, :width], level[:, :width]
 
-        def make_h(t):
-            b, i = divmod(t, 4)
-            cuts = FIRST_CUTS if t == 0 else LATER_CUTS
-            rows = slice(P * t, P * (t + 1))
+        def cosine_of(t, phase, target):
+            size = ring.tile([P, 512], F32, name="size")
+            width = target.shape[1]
+            nc.scalar.activation(size[:, :width], phase, ACT.Abs, bias=b1_sb[:, t // 4, t % 4:t % 4 + 1])
+            nc.scalar.activation(target, size[:, :width], ACT.Sin, bias=half_pi[:], scale=-1.0)
+
+        def first_tile():
+            prepare_w2(0)
+            cosine = placed("cosine0", [P, S], F32, ARENA)
+            h = ring.tile([P, S], F32, name="h")
+            for lo, hi in zip(FIRST_CUTS, FIRST_CUTS[1:]):
+                phase, level = products(0, lo, hi)
+                cosine_of(0, phase, cosine[:, lo:hi])
+                nc.vector.tensor_tensor(h[:, lo:hi], level, cosine[:, lo:hi], ALU.mult)
+                nc.vector.tensor_tensor(pages[0][:].indirect(put[:, lo // 16:hi // 16]), h[:, lo:hi],
+                                        wgs_sb[:, lo:hi], ALU.mult)
+
+        def weighted_h(t):
             prepare_w2(t)
-            h = ring.tile([P, S], F32, name="h", bufs=3)
-            cosines = [placed("cosine%d%d" % (t, n), [P, 512], F32, ARENA + 4 * t + 2 * n) for n in range(2)]
-            for lo, hi in zip(cuts, cuts[1:]):
-                cols = slice(lo, hi)
-                width = hi - lo
-                phase = psum.tile([P, 512], F32, name="bank_a")
-                level = psum.tile([P, 512], F32, name="bank_b")
-                for a in range(2):
-                    nc.tensor.matmul_mx(out=phase[:, :width], lhsT=w1_codes[t][:, P * a:P * (a + 1)].bitcast(FP8X4),
-                                        lhsT_scale=w1_sc[:, t, P * a:P * (a + 1)], rhs=v_codes[a][:, cols].bitcast(FP8X4),
-                                        rhs_scale=v_sc[4 * a:P, cols], start=(a == 0), stop=(a == 1))
-                for a in range(2):
-                    nc.tensor.matmul_mx(out=level[:, :width], lhsT=w2_codes[:, t, P * a:P * (a + 1)].bitcast(FP8X4),
-                                        lhsT_scale=w2_sc[4 * a:P, rows], rhs=v_codes[a][:, cols].bitcast(FP8X4),
-                                        rhs_scale=v_sc[4 * a:P, cols], start=(a == 0), stop=(a == 1))
-                size = ring.tile([P, 512], F32, name="size")
-                cosine = cosines[lo // 512][:, lo % 512:lo % 512 + width]
-                nc.scalar.activation(size[:, :width], phase[:, :width], ACT.Abs, bias=b1_sb[:, b, i:i + 1])
-                nc.scalar.activation(cosine, size[:, :width], ACT.Sin, bias=half_pi[:], scale=-1.0)
-                nc.vector.tensor_tensor(h[:, cols], level[:, :width], cosine, ALU.mult)
-                if t == 0:
-                    scatter(0, h, lo, hi)
-            return h
+            cosine = placed("cosine%d" % t, [P, S], F32, ARENA + 4 * t)
+            h = ring.tile([P, S], F32, name="h")
+            weighted = ring.tile([P, S], F32, name="weighted")
+            if t > 1:
+                level_sb = ring.tile([P, S], F32, name="level_sb")
+            for lo, hi in zip(LATER_CUTS, LATER_CUTS[1:]):
+                phase, level = products(t, lo, hi)
+                cosine_of(t, phase, cosine[:, lo:hi])
+                if t == 1:
+                    nc.vector.tensor_tensor(h[:, lo:hi], level, cosine[:, lo:hi], ALU.mult)
+                else:
+                    nc.scalar.copy(out=level_sb[:, lo:hi], in_=level)
+            engine = nc.vector if t == 1 else nc.gpsimd
+            for lo, hi in zip(LATER_CUTS, LATER_CUTS[1:]):
+                if t > 1:
+                    engine.tensor_tensor(h[:, lo:hi], level_sb[:, lo:hi], cosine[:, lo:hi], ALU.mult)
+            for lo, hi in zip(LATER_CUTS, LATER_CUTS[1:]):
+                engine.tensor_tensor(weighted[:, lo:hi], h[:, lo:hi], wgs_sb[:, lo:hi], ALU.mult)
+            return weighted
 
         def gather(t, x, lo, hi):
-            nc.vector.tensor_tensor(x, pages[t % 2][:].indirect(get[:, lo // 16:hi // 16]), wgt_sb[:, lo:hi], ALU.mult)
+            nc.vector.tensor_tensor(x, pages[t % 3][:].indirect(get[:, lo // 16:hi // 16]), wgt_sb[:, lo:hi], ALU.mult)
 
         def add_lens(b, u, x, lo):
             turned = psum.tile([P, 512], F32, name="bank_c")
@@ -243,13 +266,14 @@ def tile_list_dome_projector_blend_kernel(
         z_codes = [keep.tile([P, M], U32, name="z_codes%d" % b, align_bytes=64) for b in range(2)]
         z_sc = [keep.tile([P, M], U8, name="z_sc%d" % b, align_bytes=64) for b in range(2)]
         chunks = list(zip(M_CUTS, M_CUTS[1:]))
-        last_words = [keep.tile([P, 2, hi - lo], F32, name="last_words%d" % lo, align_bytes=64) for lo, hi in chunks]
+        last_words = [shared.tile([P, 2, hi - lo], F32, name="last_words%d" % lo, offset=8 * KIB + 8 * lo, align_bytes=64)
+                      for lo, hi in chunks]
         x = {}
         first_pairs = {}
-        make_h(0)
+        first_tile()
         load_lens(0)
         for t in range(1, 8):
-            h = make_h(t)
+            weighted = weighted_h(t)
             if t == 1:
                 nc.vector.tensor_scalar(b4_shift[:], b4_sb[:], 0.5, -math.pi / 4, ALU.mult, ALU.add)
             if t in (1, 2):
@@ -259,9 +283,9 @@ def tile_list_dome_projector_blend_kernel(
                 load_lens(1)
             done = t - 2
             if done >= 0:
-                x[done % 2] = placed("x%d" % done, [P, M], F32, ARENA + 4 * done + 6)
+                x[done % 2] = placed("x%d" % done, [P, M], F32, ARENA + 4 * t)
                 gather(done, x[done % 2][:], 0, M)
-            scatter(t, h, 0, S)
+            nc.vector.tensor_copy(pages[t % 3][:].indirect(put[:]), weighted[:])
             if done in (1, 3, 5):
                 b, u = done // 4, done // 2 % 2
                 for lo in range(0, M, 256):

@@ -21,8 +21,7 @@ ALU = mybir.AluOpType
 P = 128
 KIB = 1024
 FIRST_CUTS = (0, 256, 512, 1024)
-LATER_CUTS = (0, 512, 1024)
-M_CUTS = (0, 256, 512, 768, 896, 1024)
+M_CUTS = (0, 128, 384, 640, 896, 1024)
 
 
 def tile_list_dome_projector_blend_kernel(
@@ -113,18 +112,33 @@ def tile_list_dome_projector_blend_kernel(
 
         w1_codes = {}
         w1_sc = keep.tile([P, 8, 2 * P], U8, name="w1_sc", align_bytes=64)
-        w2_codes = placed("w2_codes", [P, 8, 2 * P], U32, 0)
-        w2_sc = keep.tile([P, H], U8, name="w2_sc", align_bytes=64)
+        w2_codes = placed("w2_codes", [P, 4, 2 * P], U32, 0)
+        w2_sc = keep.tile([P, 512], U8, name="w2_sc", align_bytes=64)
+        w2_sc_late = keep.tile([P, 512], U8, name="w2_sc_late", align_bytes=64)
 
         def prepare_w1(t):
             b, i = divmod(t, 4)
             grouped = ring.tile([P, 2, 512], BF16, name="w1_grouped", bufs=3, align_bytes=64)
-            w1_codes[t] = placed("w1_codes%d" % t, [P, 2 * P], U32, 136 + t if t < 2 else 16 + t)
+            w1_codes[t] = placed("w1_codes%d" % t, [P, 2 * P], U32, 136 + t if t < 2 else 16 + t)[:]
             for a in range(2):
                 nc.scalar.copy(out=grouped[:, a, :].rearrange("p (m j) -> p m j", j=4),
                                in_=w1_raw[(a, b)][:].rearrange("p j (m i) -> p i m j", i=4)[:, i])
-            nc.vector.quantize_mx(out=w1_codes[t][:].bitcast(FP8X4), scales=w1_sc[:, t, :],
+            nc.vector.quantize_mx(out=w1_codes[t].bitcast(FP8X4), scales=w1_sc[:, t, :],
                                   in_=grouped[:].rearrange("p a c -> p (a c)"))
+
+        late_grouped = placed("late_grouped", [P, 4, 2, 512], BF16, 140)
+
+        def round_late_w1(a):
+            nc.scalar.copy(out=late_grouped[:].rearrange("p i a (m j) -> p a m j i", j=4)[:, a],
+                           in_=w1_raw[(a, 1)][:].rearrange("p j (m i) -> p m j i", i=4))
+
+        def quantise_late_w1():
+            codes = placed("w1_codes_late", [P, 4, 2 * P], U32, 20)
+            nc.vector.quantize_mx(out=codes[:].rearrange("p i c -> p (i c)").bitcast(FP8X4),
+                                  scales=w1_sc[:, 4:8, :].rearrange("p i c -> p (i c)"),
+                                  in_=late_grouped[:].rearrange("p i a c -> p (i a c)"))
+            for i in range(4):
+                w1_codes[4 + i] = codes[:, i, :]
 
         def prepare_w2(t):
             b, i = divmod(t, 4)
@@ -137,8 +151,9 @@ def tile_list_dome_projector_blend_kernel(
         nc.vector.tensor_copy(v_sc[:], tab_sc[:].indirect(pick[:]))
         v_codes = [placed("v_codes0", [P, S], U32, 96), placed("v_codes1", [P, S], U32, 100)]
         nc.vector.tensor_copy(v_codes[0][:], tab[0][:].indirect(pick[:]))
-        nc.vector.tensor_copy(out=w2_sc[:].rearrange("p (b i m) -> p b i m", b=2, i=4),
-                              in_=w2_sc_raw[:].rearrange("p (b m i) -> p b i m", b=2, i=4))
+        nc.vector.tensor_copy(out=w2_sc[:].rearrange("p (i m) -> p i m", i=4),
+                              in_=w2_sc_raw[:, :512].rearrange("p (m i) -> p i m", i=4))
+        nc.vector.tensor_copy(out=w2_sc_late[:].bitcast(I32), in_=w2_sc_raw[:, 512:].bitcast(I32))
         for lo, hi in zip(FIRST_CUTS, FIRST_CUTS[1:]):
             nc.vector.tensor_copy(v_codes[1][:, lo:hi], tab[1][:].indirect(pick[:, lo // 16:hi // 16]))
 
@@ -155,61 +170,101 @@ def tile_list_dome_projector_blend_kernel(
 
         ARENA = 104
 
-        def products(t, lo, hi):
-            cols = slice(lo, hi)
-            width = hi - lo
-            phase = psum.tile([P, 512], F32, name="bank_a")
-            level = psum.tile([P, 512], F32, name="bank_b")
+        def product(tag, codes, scales, lo, hi):
+            bank = psum.tile([P, 512], F32, name=tag)
             for a in range(2):
-                nc.tensor.matmul_mx(out=phase[:, :width], lhsT=w1_codes[t][:, P * a:P * (a + 1)].bitcast(FP8X4),
-                                    lhsT_scale=w1_sc[:, t, P * a:P * (a + 1)],
-                                    rhs=v_codes[a][:, cols].bitcast(FP8X4),
-                                    rhs_scale=v_sc[4 * a:P, cols], start=(a == 0), stop=(a == 1))
-            for a in range(2):
-                nc.tensor.matmul_mx(out=level[:, :width], lhsT=w2_codes[:, t, P * a:P * (a + 1)].bitcast(FP8X4),
-                                    lhsT_scale=w2_sc[4 * a:P, P * t:P * (t + 1)],
-                                    rhs=v_codes[a][:, cols].bitcast(FP8X4),
-                                    rhs_scale=v_sc[4 * a:P, cols], start=(a == 0), stop=(a == 1))
-            return phase[:, :width], level[:, :width]
+                nc.tensor.matmul_mx(out=bank[:, :hi - lo], lhsT=codes[:, P * a:P * (a + 1)].bitcast(FP8X4),
+                                    lhsT_scale=scales[a], rhs=v_codes[a][:, lo:hi].bitcast(FP8X4),
+                                    rhs_scale=v_sc[4 * a:P, lo:hi], start=(a == 0), stop=(a == 1))
+            return bank[:, :hi - lo]
 
-        def cosine_of(t, phase, target):
-            size = ring.tile([P, 512], F32, name="size")
-            width = target.shape[1]
-            nc.scalar.activation(size[:, :width], phase, ACT.Abs, bias=b1_sb[:, t // 4, t % 4:t % 4 + 1])
-            nc.scalar.activation(target, size[:, :width], ACT.Sin, bias=half_pi[:], scale=-1.0)
+        def phase_of(t, lo, hi):
+            return product("bank_a", w1_codes[t], [w1_sc[:, t, P * a:P * (a + 1)] for a in range(2)], lo, hi)
+
+        def level_of(t, lo, hi):
+            return product("bank_b", w2_codes[:, t, :], [w2_sc[4 * a:P, P * t:P * (t + 1)] for a in range(2)], lo, hi)
+
+        def fold(t, size, lo, hi):
+            nc.scalar.activation(size[:, lo:hi], phase_of(t, lo, hi), ACT.Abs, bias=b1_sb[:, t // 4, t % 4:t % 4 + 1])
+
+        def cosine_of(size, cosine, lo, hi):
+            nc.scalar.activation(cosine[:, lo:hi], size[:, lo:hi], ACT.Sin, bias=half_pi[:], scale=-1.0)
+
+        def scatter(t, left, right, lo, hi):
+            nc.vector.tensor_tensor(pages[t % 3][:].indirect(put[:, lo // 16:hi // 16]), left[:, lo:hi],
+                                    right[:, lo:hi], ALU.mult)
 
         def first_tile():
             prepare_w2(0)
+            size = ring.tile([P, S], F32, name="size", bufs=1)
             cosine = placed("cosine0", [P, S], F32, ARENA)
             h = ring.tile([P, S], F32, name="h")
             for lo, hi in zip(FIRST_CUTS, FIRST_CUTS[1:]):
-                phase, level = products(0, lo, hi)
-                cosine_of(0, phase, cosine[:, lo:hi])
-                nc.vector.tensor_tensor(h[:, lo:hi], level, cosine[:, lo:hi], ALU.mult)
-                nc.vector.tensor_tensor(pages[0][:].indirect(put[:, lo // 16:hi // 16]), h[:, lo:hi],
-                                        wgs_sb[:, lo:hi], ALU.mult)
+                fold(0, size, lo, hi)
+                cosine_of(size, cosine, lo, hi)
+                nc.vector.tensor_tensor(h[:, lo:hi], level_of(0, lo, hi), cosine[:, lo:hi], ALU.mult)
+                scatter(0, h, wgs_sb, lo, hi)
 
-        def weighted_h(t):
+        def size_tile(t):
+            if 3 <= t <= 6:
+                return placed("size%d" % t, [P, S], F32, ARENA + 4 * (t + 1))
+            return ring.tile([P, S], F32, name="size", bufs=1)
+
+        def early_tile(t):
             prepare_w2(t)
-            cosine = placed("cosine%d" % t, [P, S], F32, ARENA + 4 * t)
+            size = size_tile(t)
+            halves = [placed("cosine%d%d" % (t, n), [P, 512], F32, ARENA + 4 * t + 2 * (1 - n)) for n in range(2)]
             h = ring.tile([P, S], F32, name="h")
-            weighted = ring.tile([P, S], F32, name="weighted")
-            if t > 1:
-                level_sb = ring.tile([P, S], F32, name="level_sb")
-            for lo, hi in zip(LATER_CUTS, LATER_CUTS[1:]):
-                phase, level = products(t, lo, hi)
-                cosine_of(t, phase, cosine[:, lo:hi])
-                if t == 1:
-                    nc.vector.tensor_tensor(h[:, lo:hi], level, cosine[:, lo:hi], ALU.mult)
-                else:
-                    nc.scalar.copy(out=level_sb[:, lo:hi], in_=level)
-            engine = nc.vector if t == 1 else nc.gpsimd
-            for lo, hi in zip(LATER_CUTS, LATER_CUTS[1:]):
-                if t > 1:
-                    engine.tensor_tensor(h[:, lo:hi], level_sb[:, lo:hi], cosine[:, lo:hi], ALU.mult)
-            for lo, hi in zip(LATER_CUTS, LATER_CUTS[1:]):
-                engine.tensor_tensor(weighted[:, lo:hi], h[:, lo:hi], wgs_sb[:, lo:hi], ALU.mult)
-            return weighted
+            levels = []
+            for lo in (0, 512):
+                fold(t, size, lo, lo + 512)
+                levels.append(level_of(t, lo, lo + 512))
+            for n in (1, 0):
+                cosine_of(size[:, 512 * n:512 * (n + 1)], halves[n], 0, 512)
+            for n in (1, 0):
+                nc.vector.tensor_tensor(h[:, 512 * n:512 * (n + 1)], levels[n], halves[n][:], ALU.mult)
+            return h, wgs_sb
+
+        wgs_turned = keep.tile([P, 8, 8], F32, name="wgs_turned")
+
+        def turn_wgs():
+            for half in range(2):
+                bank = psum.tile([P, 512], F32, name="bank_c")
+                for n in range(4):
+                    jt = 4 * half + n
+                    nc.tensor.transpose(bank[:, P * n:P * (n + 1)], wgs_sb[:, P * jt:P * (jt + 1)], ident[:])
+                nc.scalar.copy(out=wgs_turned[:, 4 * half:4 * half + 4, :],
+                               in_=bank[:].rearrange("j (n g s) -> j n g s", n=4, g=8)[:, :, :, 0])
+
+        late_level = {}
+
+        def weigh_late_level(jt):
+            bank = psum.tile([P, 512], F32, name="bank_d")
+            cols = slice(P * jt, P * (jt + 1))
+            for a in range(2):
+                nc.tensor.matmul_mx(out=bank[:], lhsT=v_codes[a][:, cols].bitcast(FP8X4),
+                                    lhsT_scale=v_sc[4 * a:P, cols], rhs=w2_raw[1][:, a, :].bitcast(FP8X4),
+                                    rhs_scale=w2_sc_late[4 * a:P, :], start=(a == 0), stop=(a == 1))
+            weighted = placed("late_level%d" % jt, [P, 4, P], F32, (4, 6, 16, 24, 26, 28, 30, 138)[jt])
+            for g in range(8):
+                nc.scalar.activation(weighted[:, :, 16 * g:16 * (g + 1)],
+                                     bank[:, 64 * g:64 * (g + 1)].rearrange("j (p i) -> j i p", i=4),
+                                     ACT.Copy, scale=wgs_turned[:, jt, g:g + 1])
+            late_level[jt] = weighted
+
+        def late_tile(t):
+            weighted = ring.tile([P, S], F32, name="h")
+            for half in range(2):
+                bank = psum.tile([P, 512], F32, name="bank_b")
+                for n in range(4):
+                    nc.tensor.transpose(bank[:, P * n:P * (n + 1)], late_level[4 * half + n][:, t - 4, :], ident[:])
+                nc.scalar.copy(out=weighted[:, 512 * half:512 * (half + 1)], in_=bank[:])
+            size = size_tile(t)
+            cosine = ring.tile([P, S], F32, name="cosine", align_bytes=64)
+            for lo in (0, 512):
+                fold(t, size, lo, lo + 512)
+            cosine_of(size, cosine, 0, S)
+            return cosine, weighted
 
         def gather(t, x, lo, hi):
             nc.vector.tensor_tensor(x, pages[t % 3][:].indirect(get[:, lo // 16:hi // 16]), wgt_sb[:, lo:hi], ALU.mult)
@@ -257,63 +312,78 @@ def tile_list_dome_projector_blend_kernel(
                 nc.scalar.activation(half[:, width * nt:width * (nt + 1)], banks[nt // per_bank][:, col:col + width],
                                      ACT.Sin, bias=b4_shift[:, nt:nt + 1], scale=0.5)
             square = ring.tile([P, 3 * 256], F32, name="square")
-            nc.scalar.activation(square[:, :3 * width], half[:, :3 * width], ACT.Square)
+            nc.vector.tensor_tensor(square[:, :3 * width], half[:, :3 * width], half[:, :3 * width], ALU.mult)
             result = ring.tile([P, 3 * 256], F32, name="result", bufs=3)
             nc.vector.tensor_scalar(result[:, :3 * width], square[:, :3 * width], -2.0, 1.0, ALU.mult, ALU.add)
             nc.sync.dma_start(out=out[:, lo:hi].rearrange("(t p) m -> p t m", p=P),
                               in_=result[:, :3 * width].rearrange("p (t m) -> p t m", t=3))
 
-        z_codes = [keep.tile([P, M], U32, name="z_codes%d" % b, align_bytes=64) for b in range(2)]
+        z_codes = {1: keep.tile([P, M], U32, name="z_codes1", align_bytes=64)}
+        z_early = placed("z_early", [P, 4 * M], BF16, 140)
         z_sc = [keep.tile([P, M], U8, name="z_sc%d" % b, align_bytes=64) for b in range(2)]
         chunks = list(zip(M_CUTS, M_CUTS[1:]))
         last_words = [shared.tile([P, 2, hi - lo], F32, name="last_words%d" % lo, offset=8 * KIB + 8 * lo, align_bytes=64)
                       for lo, hi in chunks]
         x = {}
         first_pairs = {}
+
+        def finish_pair(done):
+            b, u = done // 4, done // 2 % 2
+            for lo in range(0, M, 256):
+                pairs = add_lens(b, u, x, lo)
+                if u == 0:
+                    first_pairs[lo] = pairs
+                if done == 3:
+                    words = turn_back((first_pairs[lo], pairs))
+                    nc.scalar.copy(out=z_early[:].bitcast(F32)[:, 2 * lo:2 * lo + 512].rearrange("p (m u) -> p m u", u=2),
+                                   in_=words[:].rearrange("p (u m) -> p m u", u=2))
+                if done == 5 and lo % 512 == 256:
+                    words = turn_back((first_pairs[lo - 256], pairs))
+                    for (start, end), target in zip(chunks, last_words):
+                        first, last = max(start, lo - 256), min(end, lo + 256)
+                        if first < last:
+                            nc.scalar.copy(out=target[:, 0, first - start:last - start],
+                                           in_=words[:, first - lo + 256:last - lo + 256])
+
+        x_last = placed("x_last", [P, 2 * M + 512], F32, ARENA)
         first_tile()
         load_lens(0)
         for t in range(1, 8):
-            weighted = weighted_h(t)
+            factors = early_tile(t) if t < 4 else late_tile(t)
             if t == 1:
                 nc.vector.tensor_scalar(b4_shift[:], b4_sb[:], 0.5, -math.pi / 4, ALU.mult, ALU.add)
+                turn_wgs()
             if t in (1, 2):
-                prepare_w1(2 * t + 2)
-                prepare_w1(2 * t + 3)
+                round_late_w1(t - 1)
+                for jt in range(4 * t - 4, 4 * t):
+                    weigh_late_level(jt)
             if t == 2:
+                quantise_late_w1()
                 load_lens(1)
+            if t in (4, 6):
+                finish_pair(t - 3)
+            if t == 7:
+                z_codes[0] = ring.tile([P, M], U32, name="cosine", align_bytes=64)
+                quantise_z(0, z_early, 0, M)
             done = t - 2
             if done >= 0:
-                x[done % 2] = placed("x%d" % done, [P, M], F32, ARENA + 4 * t)
+                x[done % 2] = placed("x%d" % done, [P, M], F32, ARENA + 4 * t - (2 if t < 4 else 0))
                 gather(done, x[done % 2][:], 0, M)
-            nc.vector.tensor_copy(pages[t % 3][:].indirect(put[:]), weighted[:])
-            if done in (1, 3, 5):
-                b, u = done // 4, done // 2 % 2
-                for lo in range(0, M, 256):
-                    pairs = add_lens(b, u, x, lo)
-                    if u == 0:
-                        first_pairs[lo] = pairs
-                    if done == 3:
-                        words = turn_back((first_pairs[lo], pairs))
-                        z = ring.tile([P, 1024], BF16, name="z", align_bytes=64)
-                        nc.scalar.copy(out=z[:].bitcast(F32).rearrange("p (m u) -> p m u", u=2),
-                                       in_=words[:].rearrange("p (u m) -> p m u", u=2))
-                        quantise_z(0, z, lo, lo + 256)
-                    if done == 5 and lo % 512 == 256:
-                        words = turn_back((first_pairs[lo - 256], pairs))
-                        for (start, end), target in zip(chunks, last_words):
-                            if start // 512 == lo // 512:
-                                nc.scalar.copy(out=target[:, 0, :], in_=words[:, start % 512:start % 512 + end - start])
+            if t == 7:
+                gather(6, x_last[:, :M], 0, M)
+            scatter(t, factors[0], factors[1], 0, S)
+        finish_pair(5)
 
-        bank_tags = (("bank_a", "bank_b"), ("bank_a", "bank_b"), ("bank_c", "bank_c"), ("bank_d",), ("bank_d",))
+        bank_tags = (("bank_a",), ("bank_b", "bank_a"), ("bank_b", "bank_c"), ("bank_c", "bank_d"), ("bank_d",))
         for c, (lo, hi) in enumerate(chunks):
             width = hi - lo
-            x_pair = placed("x_pair%d" % c, [P, 2, 256], F32, ARENA + 2 * (c % 4))
-            for e in range(2):
-                gather(6 + e, x_pair[:, e, :width], lo, hi)
+            start = M + 256 * (c % 2)
+            gather(7, x_last[:, start:start + width], lo, hi)
+            x_pair = x_last[:, lo:2 * start - lo].rearrange("p (e s) -> p e s", e=2)
             nc.vector.tensor_tensor(last_words[c][:, 1, :].bitcast(BF16).rearrange("p (m e) -> p m e", e=2),
                                     x_pair[:, :, :width].rearrange("p e m -> p m e"),
                                     lens_sb[(1, 1)][:, :, lo:hi].rearrange("p e m -> p m e"), ALU.add)
-            z = placed("z_last%d" % c, [P, 1024], BF16, ARENA + 2 * ((c + 2) % 4))
+            z = ring.tile([P, 1024], BF16, name="z", align_bytes=64)
             nc.scalar.copy(out=z[:].bitcast(F32)[:, :2 * width].rearrange("p (m u) -> p m u", u=2),
                            in_=last_words[c][:].rearrange("p u m -> p m u"))
             quantise_z(1, z, lo, hi)

import math
from contextlib import ExitStack

import concourse.mybir as mybir
from concourse.masks import make_identity

T, S, M, T2, K, H, N = 4096, 1024, 1024, 2048, 1024, 1024, 384
FLOPS = 2 * (2 * K * H * S + H * N * M)

F32 = mybir.dt.float32
BF16 = mybir.dt.bfloat16
I32 = mybir.dt.int32
U32 = mybir.dt.uint32
U16 = mybir.dt.uint16
U8 = mybir.dt.uint8
FP8X4 = mybir.dt.float8_e4m3fn_x4
FP4X4 = mybir.dt.float4_e2m1fn_x4
ACT = mybir.ActivationFunctionType
ALU = mybir.AluOpType

P = 128
KIB = 1024
FIRST_CUTS = (0, 256, 512, 1024)
M_CUTS = (0, 128, 384, 640, 896, 1024)


def tile_list_dome_projector_blend_kernel(
    tc, tab_words, tab_scales, offs, offs2, offs3, w1, b1, w2_words, w2_scales,
    wgs, wgt, lens, w4_words, w4_scales, b4, out,
):
    nc = tc.nc
    with ExitStack() as ctx:
        lists = ctx.enter_context(tc.tile_pool(name="lists", bufs=1))
        keep = ctx.enter_context(tc.tile_pool(name="keep", bufs=1))
        shared = ctx.enter_context(tc.tile_pool(name="shared", bufs=1))
        ring = ctx.enter_context(tc.tile_pool(name="ring", bufs=2))
        psum = ctx.enter_context(tc.psum_pool(name="psum", bufs=2))

        def placed(name, shape, dtype, kib):
            return shared.tile(shape, dtype, name=name, offset=kib * KIB, align_bytes=64)

        pick = lists.tile([P, S // 16], U16, name="pick")
        put = lists.tile([P, S // 16], U16, name="put")
        get = lists.tile([P, M // 16], U16, name="get")

        tab = [placed("tab%d" % a, [P, T], U32, 16 * a) for a in range(2)]
        w1_raw = {(a, b): placed("w1_raw%d%d" % (a, b), [P, 4, 512], F32, 32 + 8 * (2 * b + a))
                  for a in range(2) for b in range(2)}
        w2_raw = [placed("w2_raw%d" % b, [P, 2, 512], U32, 80 + 4 * b) for b in range(2)]
        pages = [placed("page%d" % n, [P, T2], F32, kib) for n, kib in enumerate((64, 72, 88))]

        tab_sc = placed("tab_sc", [P, T], U8, 96)
        w2_sc_raw = placed("w2_sc_raw", [P, H], U8, 100)
        w4_sc = keep.tile([P, 2, N], U8, name="w4_sc", align_bytes=64)
        w4_codes = keep.tile([P, 2, 2 * N], U8, name="w4_codes", align_bytes=64)
        wgs_sb = keep.tile([P, S], F32, name="wgs_sb")
        wgt_sb = keep.tile([P, M], F32, name="wgt_sb")
        b1_sb = keep.tile([P, 2, 4], F32, name="b1_sb")
        b4_sb = keep.tile([P, 3], F32, name="b4_sb")
        b4_shift = keep.tile([P, 3], F32, name="b4_shift")
        ones = keep.tile([P, 1], F32, name="ones")
        half_pi = keep.tile([P, 1], F32, name="half_pi")
        ident = keep.tile([P, P], F32, name="ident")

        def load_w1(a, b):
            rows = w1[512 * a:512 * (a + 1), 512 * b:512 * (b + 1)]
            nc.sync.dma_start(out=w1_raw[(a, b)][:], in_=rows.rearrange("(p j) c -> p j c", j=4))

        def load_w2(b):
            words = w2_words.rearrange("a p c i -> p a (c i)").bitcast(I32)
            nc.sync.dma_start(out=w2_raw[b][:].bitcast(I32), in_=words[:, :, 512 * b:512 * (b + 1)])

        nc.vector.memset(tab_sc[:].bitcast(I32), 0)
        nc.vector.memset(w2_sc_raw[:].bitcast(I32), 0)
        nc.vector.memset(w4_sc[:].rearrange("p a n -> p (a n)").bitcast(I32), 0)
        def load_tab(a):
            nc.sync.dma_start(out=tab[a][:].bitcast(I32),
                              in_=tab_words[a].rearrange("p t i -> p (t i)").bitcast(I32))

        load_w1(0, 0)
        load_w1(1, 0)
        for q in range(4):
            nc.sync.dma_start(out=tab_sc[32 * q:32 * q + 8, :].bitcast(I32),
                              in_=tab_scales[:, 4 * q:4 * q + 4, :].bitcast(I32))
        nc.sync.dma_start(pick[:], offs)
        load_tab(0)
        for q in range(4):
            nc.sync.dma_start(out=w2_sc_raw[32 * q:32 * q + 8, :].bitcast(I32),
                              in_=w2_scales[:, 4 * q:4 * q + 4, :].bitcast(I32))
        load_tab(1)
        load_w2(0)
        nc.sync.dma_start(out=b1_sb[:], in_=b1.rearrange("(b p i) -> p b i", b=2, i=4))
        nc.sync.dma_start(put[:], offs2)
        nc.sync.dma_start(out=wgs_sb[:], in_=wgs)
        load_w1(0, 1)
        load_w1(1, 1)
        load_w2(1)
        nc.sync.dma_start(get[:], offs3)
        nc.sync.dma_start(out=wgt_sb[:], in_=wgt)
        nc.sync.dma_start(out=w4_codes[:].bitcast(I32), in_=w4_words.rearrange("a p n -> p a n").bitcast(I32))
        for q in range(4):
            nc.sync.dma_start(out=w4_sc[32 * q:32 * q + 4, :, :].bitcast(I32),
                              in_=w4_scales[:, 4 * q:4 * q + 4, :].rearrange("a r n -> r a n").bitcast(I32))
        with nc.allow_non_contiguous_dma(reason="one bias value a partition"):
            nc.sync.dma_start(out=b4_sb[:], in_=b4.rearrange("(t p) -> p t", p=P))

        nc.gpsimd.memset(ones[:], 1.0)
        nc.gpsimd.tensor_scalar(half_pi[:], ones[:], math.pi / 2, 0.0, ALU.mult, ALU.add)
        make_identity(nc, ident[:])
        for page in pages:
            nc.vector.memset(page[:], 0.0)

        w1_codes = {}
        w1_sc = keep.tile([P, 8, 2 * P], U8, name="w1_sc", align_bytes=64)
        w2_codes = placed("w2_codes", [P, 4, 2 * P], U32, 0)
        w2_sc = keep.tile([P, 512], U8, name="w2_sc", align_bytes=64)
        w2_sc_late = keep.tile([P, 512], U8, name="w2_sc_late", align_bytes=64)

        def prepare_w1(t):
            b, i = divmod(t, 4)
            grouped = ring.tile([P, 2, 512], BF16, name="w1_grouped", bufs=3, align_bytes=64)
            w1_codes[t] = placed("w1_codes%d" % t, [P, 2 * P], U32, 136 + t if t < 2 else 16 + t)[:]
            for a in range(2):
                nc.scalar.copy(out=grouped[:, a, :].rearrange("p (m j) -> p m j", j=4),
                               in_=w1_raw[(a, b)][:].rearrange("p j (m i) -> p i m j", i=4)[:, i])
            nc.vector.quantize_mx(out=w1_codes[t].bitcast(FP8X4), scales=w1_sc[:, t, :],
                                  in_=grouped[:].rearrange("p a c -> p (a c)"))

        late_grouped = placed("late_grouped", [P, 4, 2, 512], BF16, 140)

        def round_late_w1(a):
            nc.scalar.copy(out=late_grouped[:].rearrange("p i a (m j) -> p a m j i", j=4)[:, a],
                           in_=w1_raw[(a, 1)][:].rearrange("p j (m i) -> p m j i", i=4))

        def quantise_late_w1():
            codes = placed("w1_codes_late", [P, 4, 2 * P], U32, 20)
            nc.vector.quantize_mx(out=codes[:].rearrange("p i c -> p (i c)").bitcast(FP8X4),
                                  scales=w1_sc[:, 4:8, :].rearrange("p i c -> p (i c)"),
                                  in_=late_grouped[:].rearrange("p i a c -> p (i a c)"))
            for i in range(4):
                w1_codes[4 + i] = codes[:, i, :]

        def prepare_w2(t):
            b, i = divmod(t, 4)
            nc.scalar.copy(out=w2_codes[:, t, :].rearrange("p (a m) -> p a m", a=2),
                           in_=w2_raw[b][:].rearrange("p a (m i) -> p i a m", i=4)[:, i])

        prepare_w1(0)
        prepare_w1(1)
        v_sc = keep.tile([P, S], U8, name="v_sc", align_bytes=64)
        nc.vector.tensor_copy(v_sc[:], tab_sc[:].indirect(pick[:]))
        v_codes = [placed("v_codes0", [P, S], U32, 96), placed("v_codes1", [P, S], U32, 100)]
        nc.vector.tensor_copy(v_codes[0][:], tab[0][:].indirect(pick[:]))
        nc.vector.tensor_copy(out=w2_sc[:].rearrange("p (i m) -> p i m", i=4),
                              in_=w2_sc_raw[:, :512].rearrange("p (m i) -> p i m", i=4))
        nc.vector.tensor_copy(out=w2_sc_late[:].bitcast(I32), in_=w2_sc_raw[:, 512:].bitcast(I32))
        for lo, hi in zip(FIRST_CUTS, FIRST_CUTS[1:]):
            nc.vector.tensor_copy(v_codes[1][:, lo:hi], tab[1][:].indirect(pick[:, lo // 16:hi // 16]))

        prepare_w1(2)
        prepare_w1(3)
        lens_sb = {}

        def load_lens(b):
            rows = lens[512 * b:512 * (b + 1), :].rearrange("(p i) m -> p i m", i=4)
            for u in range(2):
                pair = placed("lens%d%d" % (b, u), [P, 2, M], F32, 32 + 8 * (2 * b + u))
                nc.sync.dma_start(out=pair[:], in_=rows[:, 2 * u:2 * u + 2, :])
                lens_sb[(b, u)] = pair

        ARENA = 104

        def product(tag, codes, scales, lo, hi):
            bank = psum.tile([P, 512], F32, name=tag)
            for a in range(2):
                nc.tensor.matmul_mx(out=bank[:, :hi - lo], lhsT=codes[:, P * a:P * (a + 1)].bitcast(FP8X4),
                                    lhsT_scale=scales[a], rhs=v_codes[a][:, lo:hi].bitcast(FP8X4),
                                    rhs_scale=v_sc[4 * a:P, lo:hi], start=(a == 0), stop=(a == 1))
            return bank[:, :hi - lo]

        def phase_of(t, lo, hi):
            return product("bank_a", w1_codes[t], [w1_sc[:, t, P * a:P * (a + 1)] for a in range(2)], lo, hi)

        def level_of(t, lo, hi):
            return product("bank_b", w2_codes[:, t, :], [w2_sc[4 * a:P, P * t:P * (t + 1)] for a in range(2)], lo, hi)

        def fold(t, size, lo, hi):
            nc.scalar.activation(size[:, lo:hi], phase_of(t, lo, hi), ACT.Abs, bias=b1_sb[:, t // 4, t % 4:t % 4 + 1])

        def cosine_of(size, cosine, lo, hi):
            nc.scalar.activation(cosine[:, lo:hi], size[:, lo:hi], ACT.Sin, bias=half_pi[:], scale=-1.0)

        def scatter(t, left, right, lo, hi):
            nc.vector.tensor_tensor(pages[t % 3][:].indirect(put[:, lo // 16:hi // 16]), left[:, lo:hi],
                                    right[:, lo:hi], ALU.mult)

        def first_tile():
            prepare_w2(0)
            size = ring.tile([P, S], F32, name="size", bufs=1)
            cosine = placed("cosine0", [P, S], F32, ARENA)
            h = ring.tile([P, S], F32, name="h")
            for lo, hi in zip(FIRST_CUTS, FIRST_CUTS[1:]):
                fold(0, size, lo, hi)
                cosine_of(size, cosine, lo, hi)
                nc.vector.tensor_tensor(h[:, lo:hi], level_of(0, lo, hi), cosine[:, lo:hi], ALU.mult)
                scatter(0, h, wgs_sb, lo, hi)

        def size_tile(t):
            if 3 <= t <= 6:
                return placed("size%d" % t, [P, S], F32, ARENA + 4 * (t + 1))
            return ring.tile([P, S], F32, name="size", bufs=1)

        def early_tile(t):
            prepare_w2(t)
            size = size_tile(t)
            halves = [placed("cosine%d%d" % (t, n), [P, 512], F32, ARENA + 4 * t + 2 * (1 - n)) for n in range(2)]
            h = ring.tile([P, S], F32, name="h")
            levels = []
            for lo in (0, 512):
                fold(t, size, lo, lo + 512)
                levels.append(level_of(t, lo, lo + 512))
            for n in (1, 0):
                cosine_of(size[:, 512 * n:512 * (n + 1)], halves[n], 0, 512)
            for n in (1, 0):
                nc.vector.tensor_tensor(h[:, 512 * n:512 * (n + 1)], levels[n], halves[n][:], ALU.mult)
            return h, wgs_sb

        wgs_turned = keep.tile([P, 8, 8], F32, name="wgs_turned")

        def turn_wgs():
            for half in range(2):
                bank = psum.tile([P, 512], F32, name="bank_c")
                for n in range(4):
                    jt = 4 * half + n
                    nc.tensor.transpose(bank[:, P * n:P * (n + 1)], wgs_sb[:, P * jt:P * (jt + 1)], ident[:])
                nc.scalar.copy(out=wgs_turned[:, 4 * half:4 * half + 4, :],
                               in_=bank[:].rearrange("j (n g s) -> j n g s", n=4, g=8)[:, :, :, 0])

        late_level = {}

        def weigh_late_level(jt):
            bank = psum.tile([P, 512], F32, name="bank_d")
            cols = slice(P * jt, P * (jt + 1))
            for a in range(2):
                nc.tensor.matmul_mx(out=bank[:], lhsT=v_codes[a][:, cols].bitcast(FP8X4),
                                    lhsT_scale=v_sc[4 * a:P, cols], rhs=w2_raw[1][:, a, :].bitcast(FP8X4),
                                    rhs_scale=w2_sc_late[4 * a:P, :], start=(a == 0), stop=(a == 1))
            weighted = placed("late_level%d" % jt, [P, 4, P], F32, (4, 6, 16, 24, 26, 28, 30, 138)[jt])
            for g in range(8):
                nc.scalar.activation(weighted[:, :, 16 * g:16 * (g + 1)],
                                     bank[:, 64 * g:64 * (g + 1)].rearrange("j (p i) -> j i p", i=4),
                                     ACT.Copy, scale=wgs_turned[:, jt, g:g + 1])
            late_level[jt] = weighted

        def late_tile(t):
            weighted = ring.tile([P, S], F32, name="h")
            for half in range(2):
                bank = psum.tile([P, 512], F32, name="bank_b")
                for n in range(4):
                    nc.tensor.transpose(bank[:, P * n:P * (n + 1)], late_level[4 * half + n][:, t - 4, :], ident[:])
                nc.scalar.copy(out=weighted[:, 512 * half:512 * (half + 1)], in_=bank[:])
            size = size_tile(t)
            cosine = ring.tile([P, S], F32, name="cosine", align_bytes=64)
            for lo in (0, 512):
                fold(t, size, lo, lo + 512)
            cosine_of(size, cosine, 0, S)
            return cosine, weighted

        def gather(t, x, lo, hi):
            nc.vector.tensor_tensor(x, pages[t % 3][:].indirect(get[:, lo // 16:hi // 16]), wgt_sb[:, lo:hi], ALU.mult)

        def add_lens(b, u, x, lo):
            turned = psum.tile([P, 512], F32, name="bank_c")
            steps = [(lens_sb[(b, u)][:, e, :], e) for e in range(2)] + [(x[e][:], e) for e in range(2)]
            steps = [(rows, e, mt) for rows, e in steps for mt in range(2)]
            for n, (rows, e, mt) in enumerate(steps):
                col = P * (2 * mt + e)
                nc.tensor.matmul(turned[:, col:col + P], lhsT=rows[:, lo + P * mt:lo + P * (mt + 1)], rhs=ident[:],
                                 start=(n == 0), stop=(n == len(steps) - 1), is_transpose=True)
            pairs = ring.tile([P, 512], BF16, name="pairs", bufs=6)
            nc.scalar.copy(out=pairs[:].rearrange("m (t p e) -> m t p e", e=2, p=P),
                           in_=turned[:].rearrange("m (t e p) -> m t p e", e=2, p=P))
            return pairs

        def turn_back(sources):
            words = psum.tile([P, 512], F32, name="bank_d")
            for n, (pairs, mt) in enumerate((pairs, mt) for pairs in sources for mt in range(2)):
                nc.tensor.transpose(words[:, P * n:P * (n + 1)], pairs[:].bitcast(F32)[:, P * mt:P * (mt + 1)],
                                    ident[:])
            return words

        def quantise_z(b, z, lo, hi):
            nc.vector.quantize_mx(out=z_codes[b][:, lo:hi].bitcast(FP8X4), scales=z_sc[b][:, lo:hi],
                                  in_=z[:, :4 * (hi - lo)])

        def last_product(lo, hi, tags):
            width = hi - lo
            banks = [psum.tile([P, 512], F32, name=tag) for tag in tags]
            per_bank = 512 // width
            for b in range(2):
                for nt in range(3):
                    col = width * (nt % per_bank)
                    nc.tensor.matmul_mx(out=banks[nt // per_bank][:, col:col + width],
                                        lhsT=w4_codes[:, b, 256 * nt:256 * (nt + 1)].bitcast(FP4X4),
                                        lhsT_scale=w4_sc[:, b, P * nt:P * (nt + 1)],
                                        rhs=z_codes[b][:, lo:hi].bitcast(FP8X4), rhs_scale=z_sc[b][:, lo:hi],
                                        start=(b == 0 and nt % per_bank == 0),
                                        stop=(b == 1 and (nt == 2 or nt % per_bank == per_bank - 1)))
            half = ring.tile([P, 3 * 256], F32, name="half")
            for nt in range(3):
                col = width * (nt % per_bank)
                nc.scalar.activation(half[:, width * nt:width * (nt + 1)], banks[nt // per_bank][:, col:col + width],
                                     ACT.Sin, bias=b4_shift[:, nt:nt + 1], scale=0.5)
            square = ring.tile([P, 3 * 256], F32, name="square")
            nc.vector.tensor_tensor(square[:, :3 * width], half[:, :3 * width], half[:, :3 * width], ALU.mult)
            result = ring.tile([P, 3 * 256], F32, name="result", bufs=3)
            nc.vector.tensor_scalar(result[:, :3 * width], square[:, :3 * width], -2.0, 1.0, ALU.mult, ALU.add)
            nc.sync.dma_start(out=out[:, lo:hi].rearrange("(t p) m -> p t m", p=P),
                              in_=result[:, :3 * width].rearrange("p (t m) -> p t m", t=3))

        z_codes = {1: keep.tile([P, M], U32, name="z_codes1", align_bytes=64)}
        z_early = placed("z_early", [P, 4 * M], BF16, 140)
        z_sc = [keep.tile([P, M], U8, name="z_sc%d" % b, align_bytes=64) for b in range(2)]
        chunks = list(zip(M_CUTS, M_CUTS[1:]))
        last_words = [shared.tile([P, 2, hi - lo], F32, name="last_words%d" % lo, offset=8 * KIB + 8 * lo, align_bytes=64)
                      for lo, hi in chunks]
        x = {}
        first_pairs = {}

        def finish_pair(done):
            b, u = done // 4, done // 2 % 2
            for lo in range(0, M, 256):
                pairs = add_lens(b, u, x, lo)
                if u == 0:
                    first_pairs[lo] = pairs
                if done == 3:
                    words = turn_back((first_pairs[lo], pairs))
                    nc.scalar.copy(out=z_early[:].bitcast(F32)[:, 2 * lo:2 * lo + 512].rearrange("p (m u) -> p m u", u=2),
                                   in_=words[:].rearrange("p (u m) -> p m u", u=2))
                if done == 5 and lo % 512 == 256:
                    words = turn_back((first_pairs[lo - 256], pairs))
                    for (start, end), target in zip(chunks, last_words):
                        first, last = max(start, lo - 256), min(end, lo + 256)
                        if first < last:
                            nc.scalar.copy(out=target[:, 0, first - start:last - start],
                                           in_=words[:, first - lo + 256:last - lo + 256])

        x_last = placed("x_last", [P, 2 * M + 512], F32, ARENA)
        first_tile()
        load_lens(0)
        for t in range(1, 8):
            factors = early_tile(t) if t < 4 else late_tile(t)
            if t == 1:
                nc.vector.tensor_scalar(b4_shift[:], b4_sb[:], 0.5, -math.pi / 4, ALU.mult, ALU.add)
                turn_wgs()
            if t in (1, 2):
                round_late_w1(t - 1)
                for jt in range(4 * t - 4, 4 * t):
                    weigh_late_level(jt)
            if t == 2:
                quantise_late_w1()
                load_lens(1)
            if t in (4, 6):
                finish_pair(t - 3)
            if t == 7:
                z_codes[0] = ring.tile([P, M], U32, name="cosine", align_bytes=64)
                quantise_z(0, z_early, 0, M)
            done = t - 2
            if done >= 0:
                x[done % 2] = placed("x%d" % done, [P, M], F32, ARENA + 4 * t - (2 if t < 4 else 0))
                gather(done, x[done % 2][:], 0, M)
            if t == 7:
                gather(6, x_last[:, :M], 0, M)
            scatter(t, factors[0], factors[1], 0, S)
        finish_pair(5)

        bank_tags = (("bank_a",), ("bank_b", "bank_a"), ("bank_b", "bank_c"), ("bank_c", "bank_d"), ("bank_d",))
        for c, (lo, hi) in enumerate(chunks):
            width = hi - lo
            start = M + 256 * (c % 2)
            gather(7, x_last[:, start:start + width], lo, hi)
            x_pair = x_last[:, lo:2 * start - lo].rearrange("p (e s) -> p e s", e=2)
            nc.vector.tensor_tensor(last_words[c][:, 1, :].bitcast(BF16).rearrange("p (m e) -> p m e", e=2),
                                    x_pair[:, :, :width].rearrange("p e m -> p m e"),
                                    lens_sb[(1, 1)][:, :, lo:hi].rearrange("p e m -> p m e"), ALU.add)
            z = ring.tile([P, 1024], BF16, name="z", align_bytes=64)
            nc.scalar.copy(out=z[:].bitcast(F32)[:, :2 * width].rearrange("p (m u) -> p m u", u=2),
                           in_=last_words[c][:].rearrange("p u m -> p m u"))
            quantise_z(1, z, lo, hi)
            last_product(lo, hi, bank_tags[c])
